import numpy as np
import ml_dtypes


def mxq(x, axis, fmt="e4m3"):
    dtype, down = {"e4m3": (ml_dtypes.float8_e4m3fn, 7), "e5m2": (ml_dtypes.float8_e5m2, 14)}[fmt]
    v = np.moveaxis(np.asarray(x, np.float32).astype(ml_dtypes.bfloat16).astype(np.float64), axis, -1)
    blocks = v.reshape(v.shape[:-1] + (-1, 32))
    amax = np.abs(blocks).max(-1, keepdims=True)
    byte = np.maximum(np.where(amax > 0, np.frexp(amax)[1] - 1 + 127, 0) - down, 1)
    scale = np.exp2(byte - 127.0)
    codes = (blocks / scale).astype(np.float32).astype(dtype).astype(np.float64)
    return np.moveaxis((codes * scale).reshape(v.shape), -1, axis)


WIDE = False


def mx_kscale(k):
    if not WIDE:
        return np.ones(k)
    levels = np.array([10, -10, 5, -5, 0])
    if k % 512:
        return np.exp2(np.random.permutation(np.resize(levels, k // 32))).repeat(32)
    a = np.empty((k // 512, 16))
    for p in range(k // 512):
        a[p, :8] = np.random.permutation(np.resize(levels, 8))
        for g in range(8):
            far = levels[np.abs(levels - a[p, g]) >= 10]
            a[p, g + 8] = far[np.random.randint(len(far))]
    return np.exp2(a.ravel()).repeat(32)


def f64(x):
    return np.asarray(x).astype(np.float64)


def striped(idx):
    return np.tile(idx.reshape(-1, 16).T, (8, 1)).astype(np.uint16)


def unstriped(offs):
    return offs[:16].T.reshape(-1).astype(np.int64)


def striped8(idx):
    return np.concatenate([x.reshape(-1, 16).T for x in idx]).astype(np.uint16)


def runs(offs, k):
    lists = np.stack([offs[16 * r : 16 * r + 16].T.reshape(-1) for r in range(8)]).astype(np.int64)
    return lists[np.arange(k) % 512 // 64]


def pack_weight(w):
    k, n = w.shape
    w = f64(np.asarray(w, np.float32).astype(ml_dtypes.bfloat16)).reshape(k // 32, 32, n)
    amax = np.abs(w).max(1)
    byte = np.clip(np.where(amax > 0, np.frexp(amax)[1] - 1 + 127 - 7, 1), 1, 254)
    scaled = (w * np.exp2(127.0 - byte)[:, None, :]).reshape(k, n).astype(np.float32)
    words = np.ascontiguousarray(scaled.reshape(k // 512, 128, 4, n).transpose(0, 1, 3, 2)).astype(ml_dtypes.float8_e4m3fn).view(np.uint8)
    return words, np.ascontiguousarray(byte.astype(np.uint8).reshape(k // 512, 16, n))


def unpack_weight(words, scales):
    g, p, n, _ = words.shape
    vals = np.ascontiguousarray(words).view(ml_dtypes.float8_e4m3fn).astype(np.float64) * np.repeat(np.exp2(scales.astype(np.float64) - 127.0), 8, axis=1)[..., None]
    return vals.transpose(0, 1, 3, 2).reshape(g * 512, n)

def planes(y):
    n, m = y.shape
    v = y.astype(np.float32).astype(ml_dtypes.bfloat16).astype(np.float64).reshape(n // 32, 32, m)
    top = np.abs(v).max(1)
    byte = np.clip(np.where(top > 0, np.frexp(top)[1] - 1 + 127 - 7, 1), 1, 254)
    codes = (v * np.exp2(127.0 - byte)[:, None, :]).reshape(n, m).astype(np.float32).astype(ml_dtypes.float8_e4m3fn).view(np.uint8)
    words = codes.reshape(n // 512, 128, 4, m).transpose(0, 1, 3, 2)
    return np.ascontiguousarray(words), np.ascontiguousarray(byte.astype(np.uint8).reshape(n // 512, 16, m))


K, T, S, H, J, G = 512, 2048, 512, 512, 512, 2048


def setup_inputs():
    n = np.random.standard_normal
    s = mx_kscale(K)[:, None]
    packed_xT = pack_weight(n((K, T)) * s)
    packed_w1 = pack_weight(n((K, H)) / np.sqrt(K) / s)
    packed_dT = pack_weight(n((K, G)) / s)
    return {
        "x_words": packed_xT[0],
        "x_scales": packed_xT[1],
        "w1_words": packed_w1[0],
        "w1_scales": packed_w1[1],
        "tab": n((H, J)).astype(np.float32),
        "gs": (np.random.uniform(0.5, 1.5, (K, 1)) * s).astype(np.float32),
        "d_words": packed_dT[0],
        "d_scales": packed_dT[1],
        "offs": striped(np.random.permutation(T)[:S]),
        "n1": striped8(np.random.randint(0, J, (8, S))),
        "n2": striped8(np.stack([np.random.permutation(S) for _ in range(8)])),
        "k1": striped8(np.random.randint(0, G, (8, H))),
        "n3": striped8(np.stack([np.random.permutation(S) for _ in range(8)])),
        "n4": striped8(np.stack([np.random.permutation(S) for _ in range(8)])),
        "n5": striped8(np.stack([np.random.permutation(S) for _ in range(8)])),
    }


def reference(x_words, x_scales, w1_words, w1_scales, tab, gs, d_words, d_scales, offs, n1, n2, k1, n3, n4, n5):
    d_k1 = unpack_weight(d_words, d_scales)[np.arange(K)[:, None], runs(k1, K)]
    xq = unpack_weight(x_words, x_scales)[:, unstriped(offs)]
    y = unpack_weight(w1_words, w1_scales).T @ xq
    z = f64(gs) * (np.maximum(y + f64(tab)[np.arange(H)[:, None], runs(n1, H)], y[np.arange(H)[:, None], runs(n2, H)]))
    h = 0.0625 * ((d_k1.T @ mxq(z, 0, "e4m3")))
    out_0 = np.maximum(h, h[np.arange(H)[:, None], runs(n3, H)]) - (np.maximum(h[np.arange(H)[:, None], runs(n4, H)], h[np.arange(H)[:, None], runs(n5, H)]))
    return (out_0,) + planes(out_0)

@@ -1,0 +1,227 @@
+from contextlib import ExitStack
+
+import concourse.mybir as mybir
+
+F32 = mybir.dt.float32
+BF16 = mybir.dt.bfloat16
+I32 = mybir.dt.int32
+U32 = mybir.dt.uint32
+U16 = mybir.dt.uint16
+U8 = mybir.dt.uint8
+FP8X4 = mybir.dt.float8_e4m3fn_x4
+ALU = mybir.AluOpType
+COPY = mybir.ActivationFunctionType.Copy
+
+P = 128
+PACK = 4
+N = 512
+TABLE = 2048
+STRIPE = 16
+FLOPS = 2 * 2 * 512 * 512 * 512
+
+Z_PIECES = ((0, 256), (256, 512))
+OUT_PIECES = ((0, 256), (256, 384), (384, 512))
+
+
+def units(pieces):
+    return [(t, 0, N) for t in range(PACK - 1)] + [(PACK - 1, a, b) for a, b in pieces]
+
+
+def tile_picked_densekindmix_none_po_kernel(
+    tc, x_words, x_scales, w1_words, w1_scales, tab, gs, d_words, d_scales,
+    offs, n1, n2, k1, n3, n4, n5, out_0, out_1, out_2,
+):
+    nc = tc.nc
+    with ExitStack() as ctx:
+        keep = ctx.enter_context(tc.tile_pool(name="keep", bufs=1))
+        psum = ctx.enter_context(tc.psum_pool(name="psum", bufs=1))
+
+        def tile(shape, dtype, name):
+            return keep.tile(shape, dtype, name=name, align_bytes=64)
+
+        def load_list(dram, name):
+            held = tile([P, N // STRIPE], U16, name)
+            nc.sync.dma_start(held[:], dram)
+            return held
+
+        def words_of(dram):
+            return dram[0].rearrange("p n t -> p (n t)").bitcast(I32)
+
+        def window(t, name):
+            return tile([P, N if t == PACK - 1 else 2 * N], F32, name)
+
+        def picked(win, lists, a, b):
+            return win[:].indirect(lists[:, a // STRIPE : b // STRIPE])
+
+        def deal(dst, src, run):
+            nc.vector.tensor_copy(
+                dst.rearrange("p (t c m) -> p c t m", t=PACK, m=run),
+                src.rearrange("p (c m t) -> p c t m", t=PACK, m=run),
+            )
+
+        xs_table = tile([P, TABLE], U8, "xs_table")
+        ds_table = tile([P, TABLE], U8, "ds_table")
+        w1s_raw = tile([P, N], U8, "w1s_raw")
+        ds_placed = tile([P, N], U8, "ds_placed")
+        nc.vector.memset(xs_table[:].bitcast(I32), 0)
+        nc.gpsimd.memset(w1s_raw[:].bitcast(I32), 0)
+        nc.vector.memset(ds_table[:].bitcast(I32), 0)
+        nc.vector.memset(ds_placed[:].bitcast(I32), 0)
+
+        offs_sb = load_list(offs, "offs_sb")
+        k1_sb = load_list(k1, "k1_sb")
+        n2_sb = load_list(n2, "n2_sb")
+        n1_sb = load_list(n1, "n1_sb")
+        n3_sb = load_list(n3, "n3_sb")
+        n4_sb = load_list(n4, "n4_sb")
+        xw_table = tile([P, TABLE], I32, "xw_table")
+        w1w_raw = tile([P, N], I32, "w1w_raw")
+        nc.scalar.dma_start(w1w_raw[:], words_of(w1_words))
+        nc.scalar.dma_start(xw_table[:], words_of(x_words))
+        for q in range(4):
+            nc.sync.dma_start(xs_table[:].bitcast(I32)[32 * q : 32 * q + 4, :], x_scales[0].bitcast(I32)[4 * q : 4 * q + 4, :])
+        for q in range(4):
+            nc.scalar.dma_start(w1s_raw[:].bitcast(I32)[32 * q : 32 * q + 4, :], w1_scales[0].bitcast(I32)[4 * q : 4 * q + 4, :])
+        nc.sync.dma_start(ds_table[:].bitcast(I32)[0:P:8, :], d_scales[0].bitcast(I32))
+        tab_rows = tab.rearrange("(p t) j -> p t j", t=PACK)
+        tab_win = []
+        for t in range(PACK):
+            tab_win.append(window(t, f"tab_win{t}"))
+            nc.sync.dma_start(tab_win[t][:, 0:N], tab_rows[:, t, :])
+        gs_sb = tile([P, PACK], F32, "gs_sb")
+        nc.sync.dma_start(gs_sb[:], gs.rearrange("(p t) o -> p (t o)", t=PACK))
+        dw_table = tile([P, TABLE], I32, "dw_table")
+        nc.sync.dma_start(dw_table[:], words_of(d_words))
+        n5_sb = load_list(n5, "n5_sb")
+
+        xs = tile([P, N], U8, "xs")
+        nc.vector.tensor_copy(xs[:], picked(xs_table, offs_sb, 0, N))
+        w1w = tile([P, N], U32, "w1w")
+        deal(w1w[:], w1w_raw[:].bitcast(U32), 4)
+        w1s = tile([P, N], U8, "w1s")
+        deal(w1s[:], w1s_raw[:], 16)
+        xw = tile([P, N], U32, "xw")
+        nc.vector.tensor_copy(xw[:], xw_table[:].bitcast(U32).indirect(offs_sb[:]))
+
+        y_win = []
+        for t in range(PACK):
+            bank = psum.tile([P, N], F32, name=f"bank{t}")
+            cols = slice(t * P, (t + 1) * P)
+            nc.tensor.matmul_mx(bank[:], w1w[:, cols].bitcast(FP8X4), w1s[:, cols], xw[:].bitcast(FP8X4), xs[:], start=True, stop=True)
+            y_win.append(window(t, f"y_win{t}"))
+            nc.scalar.copy(y_win[t][:, 0:N], bank[:])
+
+        ds_picked = tile([P, N], U8, "ds_picked")
+        nc.vector.tensor_copy(ds_picked[:], picked(ds_table, k1_sb, 0, N))
+        ds_dealt = tile([P, N], U8, "ds_dealt")
+        deal(ds_dealt[:], ds_picked[:], 16)
+        for r in range(4):
+            nc.sync.dma_start(ds_placed[:].bitcast(I32)[r:P:32, :], ds_dealt[:].bitcast(I32)[8 * r : P : 32, :])
+
+        z_bf = [tile([P, b - a, PACK], BF16, f"z_bf{a}") for a, b in Z_PIECES]
+        first = units(Z_PIECES)
+        other = {}
+        summed = {}
+
+        def fetch_other(u):
+            t, a, b = u
+            other[u] = tile([P, b - a], F32, f"other{t}_{a}")
+            nc.vector.tensor_copy(other[u][:], picked(y_win[t], n2_sb, a, b))
+
+        def fetch_sum(u):
+            t, a, b = u
+            summed[u] = tile([P, b - a], F32, f"summed{t}_{a}")
+            nc.vector.tensor_tensor(summed[u][:], picked(tab_win[t], n1_sb, a, b), y_win[t][:, a:b], ALU.add)
+
+        def finish_z(u):
+            t, a, b = u
+            larger = tile([P, b - a], F32, f"larger{t}_{a}")
+            nc.vector.tensor_tensor(larger[:], summed[u][:], other[u][:], ALU.max)
+            for (c, d), dst in zip(Z_PIECES, z_bf):
+                if a <= c and d <= b:
+                    nc.scalar.activation(dst[:, :, t], larger[:, c - a : d - a], COPY, scale=gs_sb[:, t : t + 1])
+
+        fetch_other(first[0])
+        for i, u in enumerate(first):
+            fetch_sum(u)
+            if i + 1 < len(first):
+                fetch_other(first[i + 1])
+            finish_z(u)
+
+        dw_picked = tile([P, N], U32, "dw_picked")
+        nc.vector.tensor_copy(dw_picked[:], dw_table[:].bitcast(U32).indirect(k1_sb[:]))
+        dw = tile([P, N], U32, "dw")
+        deal(dw[:], dw_picked[:], 4)
+
+        z_words = []
+        z_scales = []
+        for (a, b), src in zip(Z_PIECES, z_bf):
+            z_words.append(tile([P, b - a], U32, f"z_words{a}"))
+            z_scales.append(tile([P, b - a], U8, f"z_scales{a}"))
+            nc.vector.quantize_mx(z_words[-1][:].bitcast(FP8X4), z_scales[-1][:], src[:].rearrange("p n t -> p (n t)"))
+
+        neg_h = []
+        for t in range(PACK):
+            cols = slice(t * P, (t + 1) * P)
+            neg_h.append(window(t, f"neg_h{t}"))
+            for i, (a, b) in enumerate(Z_PIECES):
+                bank = psum.tile([P, N], F32, name=f"bank{(4 + 2 * t + i) % 8}")
+                nc.tensor.matmul_mx(bank[:, 0 : b - a], dw[:, cols].bitcast(FP8X4), ds_placed[:, cols], z_words[i][:].bitcast(FP8X4), z_scales[i][:], start=True, stop=True)
+                nc.scalar.activation(neg_h[t][:, a:b], bank[:, 0 : b - a], COPY, scale=-0.0625)
+
+        second = units(OUT_PIECES)
+        out_bf = [tile([P, b - a, PACK], BF16, f"out_bf{a}") for a, b in OUT_PIECES]
+        out_scales = tile([P, N], U8, "out_scales")
+        out_rows = out_0.rearrange("(p t) j -> p t j", t=PACK)
+        at3 = {}
+        neg_top = {}
+        less4 = {}
+        less5 = {}
+
+        def fetch3(u):
+            t, a, b = u
+            at3[u] = tile([P, b - a], F32, f"at3_{t}_{a}")
+            nc.vector.tensor_copy(at3[u][:], picked(neg_h[t], n3_sb, a, b))
+
+        def top(u):
+            t, a, b = u
+            neg_top[u] = tile([P, b - a], F32, f"neg_top{t}_{a}")
+            nc.vector.tensor_tensor(neg_top[u][:], at3[u][:], neg_h[t][:, a:b], ALU.min)
+
+        def fetch_less(u, lists, into, name):
+            t, a, b = u
+            into[u] = tile([P, b - a], F32, f"{name}_{t}_{a}")
+            nc.vector.tensor_tensor(into[u][:], picked(neg_h[t], lists, a, b), neg_top[u][:], ALU.subtract)
+
+        def finish_out(u):
+            t, a, b = u
+            result = tile([P, b - a], F32, f"result{t}_{a}")
+            nc.vector.tensor_tensor(result[:], less4[u][:], less5[u][:], ALU.min)
+            nc.sync.dma_start(out_rows[:, t, a:b], result[:])
+            for (c, d), dst in zip(OUT_PIECES, out_bf):
+                if a <= c and d <= b:
+                    nc.scalar.copy(dst[:, :, t], result[:, c - a : d - a])
+
+        def planes(i):
+            a, b = OUT_PIECES[i]
+            codes = tile([P, b - a], I32, f"out_words{a}")
+            nc.vector.quantize_mx(codes[:].bitcast(FP8X4), out_scales[:, a:b], out_bf[i][:].rearrange("p n t -> p (n t)"))
+            nc.sync.dma_start(words_of(out_1)[:, a:b], codes[:])
+
+        fetch3(second[0])
+        fetch3(second[1])
+        top(second[0])
+        for i, u in enumerate(second):
+            fetch_less(u, n4_sb, less4, "less4")
+            if i + 1 < len(second):
+                top(second[i + 1])
+            fetch_less(u, n5_sb, less5, "less5")
+            if i + 2 < len(second):
+                fetch3(second[i + 2])
+            if i > PACK - 1:
+                planes(i - PACK)
+            finish_out(u)
+        planes(len(OUT_PIECES) - 1)
+        for q in range(4):
+            queue = nc.scalar if q % 2 else nc.sync
+            queue.dma_start(out_2[0].bitcast(I32)[4 * q : 4 * q + 4, :], out_scales[:].bitcast(I32)[32 * q : 32 * q + 4, :])

@@ -63,35 +63,39 @@ def tile_picked_densekindmix_none_po_kernel(
         ds_table = tile([P, TABLE], U8, "ds_table")
         w1s_raw = tile([P, N], U8, "w1s_raw")
         ds_placed = tile([P, N], U8, "ds_placed")
-        nc.vector.memset(xs_table[:].bitcast(I32), 0)
-        nc.gpsimd.memset(w1s_raw[:].bitcast(I32), 0)
+        xw_table = tile([P, TABLE], I32, "xw_table")
+        dw_table = tile([P, TABLE], I32, "dw_table")
+        w1w_raw = tile([P, N], I32, "w1w_raw")
+        gs_sb = tile([P, PACK], F32, "gs_sb")
+        tab_rows = tab.rearrange("(p t) j -> p t j", t=PACK)
+        tab_win = [window(t, f"tab_win{t}") for t in range(PACK)]
+        nc.gpsimd.memset(xs_table[:].bitcast(I32), 0)
+        nc.vector.memset(w1s_raw[:].bitcast(I32), 0)
         nc.vector.memset(ds_table[:].bitcast(I32), 0)
         nc.vector.memset(ds_placed[:].bitcast(I32), 0)
-
+        nc.sync.dma_start(w1w_raw[:], words_of(w1_words))
         offs_sb = load_list(offs, "offs_sb")
+        nc.sync.dma_start(xs_table[:].bitcast(I32)[0 : 4, :], x_scales[0].bitcast(I32)[0 : 4, :])
+        nc.sync.dma_start(xs_table[:].bitcast(I32)[32 : 36, :], x_scales[0].bitcast(I32)[4 : 8, :])
+        nc.sync.dma_start(xs_table[:].bitcast(I32)[64 : 68, :], x_scales[0].bitcast(I32)[8 : 12, :])
+        nc.sync.dma_start(xs_table[:].bitcast(I32)[96 : 100, :], x_scales[0].bitcast(I32)[12 : 16, :])
+        nc.sync.dma_start(xw_table[:], words_of(x_words))
+        nc.sync.dma_start(w1s_raw[:].bitcast(I32)[0 : 4, :], w1_scales[0].bitcast(I32)[0 : 4, :])
+        nc.sync.dma_start(w1s_raw[:].bitcast(I32)[32 : 36, :], w1_scales[0].bitcast(I32)[4 : 8, :])
+        nc.sync.dma_start(w1s_raw[:].bitcast(I32)[64 : 68, :], w1_scales[0].bitcast(I32)[8 : 12, :])
+        nc.sync.dma_start(w1s_raw[:].bitcast(I32)[96 : 100, :], w1_scales[0].bitcast(I32)[12 : 16, :])
         k1_sb = load_list(k1, "k1_sb")
+        nc.sync.dma_start(ds_table[:].bitcast(I32)[0:P:8, :], d_scales[0].bitcast(I32))
         n2_sb = load_list(n2, "n2_sb")
         n1_sb = load_list(n1, "n1_sb")
+        nc.sync.dma_start(tab_win[0][:, 0:N], tab_rows[:, 0, :])
+        nc.sync.dma_start(tab_win[1][:, 0:N], tab_rows[:, 1, :])
+        nc.sync.dma_start(tab_win[2][:, 0:N], tab_rows[:, 2, :])
+        nc.sync.dma_start(tab_win[3][:, 0:N], tab_rows[:, 3, :])
+        nc.sync.dma_start(gs_sb[:], gs.rearrange("(p t) o -> p (t o)", t=PACK))
+        nc.sync.dma_start(dw_table[:], words_of(d_words))
         n3_sb = load_list(n3, "n3_sb")
         n4_sb = load_list(n4, "n4_sb")
-        xw_table = tile([P, TABLE], I32, "xw_table")
-        w1w_raw = tile([P, N], I32, "w1w_raw")
-        nc.scalar.dma_start(w1w_raw[:], words_of(w1_words))
-        nc.scalar.dma_start(xw_table[:], words_of(x_words))
-        for q in range(4):
-            nc.sync.dma_start(xs_table[:].bitcast(I32)[32 * q : 32 * q + 4, :], x_scales[0].bitcast(I32)[4 * q : 4 * q + 4, :])
-        for q in range(4):
-            nc.scalar.dma_start(w1s_raw[:].bitcast(I32)[32 * q : 32 * q + 4, :], w1_scales[0].bitcast(I32)[4 * q : 4 * q + 4, :])
-        nc.sync.dma_start(ds_table[:].bitcast(I32)[0:P:8, :], d_scales[0].bitcast(I32))
-        tab_rows = tab.rearrange("(p t) j -> p t j", t=PACK)
-        tab_win = []
-        for t in range(PACK):
-            tab_win.append(window(t, f"tab_win{t}"))
-            nc.sync.dma_start(tab_win[t][:, 0:N], tab_rows[:, t, :])
-        gs_sb = tile([P, PACK], F32, "gs_sb")
-        nc.sync.dma_start(gs_sb[:], gs.rearrange("(p t) o -> p (t o)", t=PACK))
-        dw_table = tile([P, TABLE], I32, "dw_table")
-        nc.sync.dma_start(dw_table[:], words_of(d_words))
         n5_sb = load_list(n5, "n5_sb")
 
         xs = tile([P, N], U8, "xs")
@@ -142,23 +146,27 @@ def tile_picked_densekindmix_none_po_kernel(
                     nc.scalar.activation(dst[:, :, t], larger[:, c - a : d - a], COPY, scale=gs_sb[:, t : t + 1])
 
         fetch_other(first[0])
-        for i, u in enumerate(first):
+        for u, following in zip(first, first[1:]):
             fetch_sum(u)
-            if i + 1 < len(first):
-                fetch_other(first[i + 1])
-            finish_z(u)
+            fetch_other(following)
+            if following != first[-1]:
+                finish_z(u)
+        fetch_sum(first[-1])
+        finish_z(first[-2])
+        finish_z(first[-1])
 
         dw_picked = tile([P, N], U32, "dw_picked")
         nc.vector.tensor_copy(dw_picked[:], dw_table[:].bitcast(U32).indirect(k1_sb[:]))
-        dw = tile([P, N], U32, "dw")
-        deal(dw[:], dw_picked[:], 4)
+        z_words = [tile([P, b - a], U32, f"z_words{a}") for a, b in Z_PIECES]
+        z_scales = [tile([P, b - a], U8, f"z_scales{a}") for a, b in Z_PIECES]
 
-        z_words = []
-        z_scales = []
-        for (a, b), src in zip(Z_PIECES, z_bf):
-            z_words.append(tile([P, b - a], U32, f"z_words{a}"))
-            z_scales.append(tile([P, b - a], U8, f"z_scales{a}"))
-            nc.vector.quantize_mx(z_words[-1][:].bitcast(FP8X4), z_scales[-1][:], src[:].rearrange("p n t -> p (n t)"))
+        def quantize_z(i):
+            nc.vector.quantize_mx(z_words[i][:].bitcast(FP8X4), z_scales[i][:], z_bf[i][:].rearrange("p n t -> p (n t)"))
+
+        dw = tile([P, N], U32, "dw")
+        quantize_z(0)
+        deal(dw[:], dw_picked[:], 4)
+        quantize_z(1)
 
         neg_h = []
         for t in range(PACK):
@@ -211,17 +219,22 @@ def tile_picked_densekindmix_none_po_kernel(
         fetch3(second[0])
         fetch3(second[1])
         top(second[0])
-        for i, u in enumerate(second):
+        top(second[1])
+        for u, ahead in zip(second, second[2:]):
             fetch_less(u, n4_sb, less4, "less4")
-            if i + 1 < len(second):
-                top(second[i + 1])
             fetch_less(u, n5_sb, less5, "less5")
-            if i + 2 < len(second):
-                fetch3(second[i + 2])
-            if i > PACK - 1:
-                planes(i - PACK)
+            fetch3(ahead)
             finish_out(u)
-        planes(len(OUT_PIECES) - 1)
+            top(ahead)
+        fetch_less(second[-2], n4_sb, less4, "less4")
+        fetch_less(second[-2], n5_sb, less5, "less5")
+        fetch_less(second[-1], n4_sb, less4, "less4")
+        finish_out(second[-2])
+        fetch_less(second[-1], n5_sb, less5, "less5")
+        planes(0)
+        finish_out(second[-1])
+        planes(1)
+        planes(2)
         for q in range(4):
             queue = nc.scalar if q % 2 else nc.sync
             queue.dma_start(out_2[0].bitcast(I32)[4 * q : 4 * q + 4, :], out_scales[:].bitcast(I32)[32 * q : 32 * q + 4, :])

@@ -1,6 +1,7 @@
 from contextlib import ExitStack
 
 import concourse.mybir as mybir
+from concourse.masks import make_identity
 
 F32 = mybir.dt.float32
 BF16 = mybir.dt.bfloat16
@@ -11,6 +12,7 @@ U8 = mybir.dt.uint8
 FP8X4 = mybir.dt.float8_e4m3fn_x4
 ALU = mybir.AluOpType
 COPY = mybir.ActivationFunctionType.Copy
+RELU = mybir.ActivationFunctionType.Relu
 
 P = 128
 PACK = 4
@@ -53,10 +55,10 @@ def tile_picked_densekindmix_none_po_kernel(
         def picked(win, lists, a, b):
             return win[:].indirect(lists[:, a // STRIPE : b // STRIPE])
 
-        def deal(dst, src, run):
+        def deal(dst, src, run, first=0, last=PACK):
             nc.vector.tensor_copy(
-                dst.rearrange("p (t c m) -> p c t m", t=PACK, m=run),
-                src.rearrange("p (c m t) -> p c t m", t=PACK, m=run),
+                dst.rearrange("p (t c m) -> p c t m", t=PACK, m=run)[:, :, first:last, :],
+                src.rearrange("p (c m t) -> p c t m", t=PACK, m=run)[:, :, first:last, :],
             )
 
         xs_table = tile([P, TABLE], U8, "xs_table")
@@ -97,6 +99,9 @@ def tile_picked_densekindmix_none_po_kernel(
         n3_sb = load_list(n3, "n3_sb")
         n4_sb = load_list(n4, "n4_sb")
         n5_sb = load_list(n5, "n5_sb")
+
+        identity = tile([P, P], F32, "identity")
+        make_identity(nc, identity[:])
 
         xs = tile([P, N], U8, "xs")
         nc.vector.tensor_copy(xs[:], picked(xs_table, offs_sb, 0, N))
@@ -165,50 +170,93 @@ def tile_picked_densekindmix_none_po_kernel(
 
         dw = tile([P, N], U32, "dw")
         quantize_z(0)
-        deal(dw[:], dw_picked[:], 4)
+        deal(dw[:], dw_picked[:], 4, 0, 1)
         quantize_z(1)
+        deal(dw[:], dw_picked[:], 4, 1, PACK)
 
-        neg_h = []
-        for t in range(PACK):
+        neg_h = [window(t, f"neg_h{t}") for t in range(PACK)]
+        blocks = [slice(c * P, (c + 1) * P) for c in range(N // P)]
+        h_turned = {}
+        gain_turned = {}
+        gap3 = {}
+        top = {}
+
+        def product(t):
             cols = slice(t * P, (t + 1) * P)
-            neg_h.append(window(t, f"neg_h{t}"))
             for i, (a, b) in enumerate(Z_PIECES):
                 bank = psum.tile([P, N], F32, name=f"bank{(4 + 2 * t + i) % 8}")
                 nc.tensor.matmul_mx(bank[:, 0 : b - a], dw[:, cols].bitcast(FP8X4), ds_placed[:, cols], z_words[i][:].bitcast(FP8X4), z_scales[i][:], start=True, stop=True)
                 nc.scalar.activation(neg_h[t][:, a:b], bank[:, 0 : b - a], COPY, scale=-0.0625)
 
+        def turn_h(t):
+            bank = psum.tile([P, N], F32, name=f"bank{(4 + 2 * t) % 8}")
+            for block in blocks:
+                nc.tensor.transpose(bank[:, block], neg_h[t][:, block], identity[:])
+            h_turned[t] = tile([P, N], F32, f"h_turned{t}")
+            nc.scalar.activation(h_turned[t][:], bank[:], COPY, scale=-1.0)
+
+        def fetch3(t):
+            h = tile([P, N], F32, f"h{t}")
+            nc.scalar.activation(h[:], neg_h[t][:, 0:N], COPY, scale=-1.0)
+            gap3[t] = tile([P, N], F32, f"gap3_{t}")
+            for a, b in Z_PIECES if t == PACK - 1 else ((0, N),):
+                nc.vector.tensor_tensor(gap3[t][:, a:b], picked(neg_h[t], n3_sb, a, b), h[:, a:b], ALU.add)
+
+        def turn_gain(t):
+            bank = psum.tile([P, N], F32, name=f"bank{(5 + 2 * t) % 8}")
+            for block in blocks:
+                nc.tensor.transpose(bank[:, block], gap3[t][:, block], identity[:])
+            gain_turned[t] = tile([P, N], F32, f"gain_turned{t}")
+            nc.scalar.activation(gain_turned[t][:], bank[:], RELU, scale=-1.0)
+
+        def make_top(t):
+            bank = psum.tile([P, N], F32, name=f"bank{(4 + 2 * t) % 8}")
+            for block in blocks:
+                nc.tensor.matmul(bank[:, block], h_turned[t][:, block], identity[:], start=True, stop=False, is_transpose=True)
+                nc.tensor.matmul(bank[:, block], gain_turned[t][:, block], identity[:], start=False, stop=True, is_transpose=True)
+            top[t] = tile([P, N], F32, f"top{t}")
+            nc.scalar.copy(top[t][:], bank[:])
+
+        product(0)
+        at3 = tile([P, N], F32, "at3")
+        nc.vector.tensor_copy(at3[:], picked(neg_h[0], n3_sb, 0, N))
+        product(1)
+        fetch3(1)
+        top[0] = tile([P, N], F32, "neg_top0")
+        nc.vector.tensor_tensor(top[0][:], at3[:], neg_h[0][:, 0:N], ALU.min)
+        for t in range(2, PACK):
+            product(t)
+            fetch3(t)
+        turn_h(1)
+        turn_gain(1)
+        for t in range(2, PACK):
+            turn_h(t)
+            turn_gain(t)
+            make_top(t - 1)
+        make_top(PACK - 1)
+
         second = units(OUT_PIECES)
-        out_bf = [tile([P, b - a, PACK], BF16, f"out_bf{a}") for a, b in OUT_PIECES]
+        out_bf = [tile([P, b - a, PACK], BF16, name) for (a, b), name in zip(OUT_PIECES, ("gap3_3", "h_turned3", "gain_turned3"))]
         out_scales = tile([P, N], U8, "out_scales")
         out_rows = out_0.rearrange("(p t) j -> p t j", t=PACK)
-        at3 = {}
-        neg_top = {}
+        result = [tile([P, 2, N], F32, f"result{pair}") for pair in range(2)]
         less4 = {}
         less5 = {}
 
-        def fetch3(u):
+        def fetch_less(u, lists, into, name, reused):
             t, a, b = u
-            at3[u] = tile([P, b - a], F32, f"at3_{t}_{a}")
-            nc.vector.tensor_copy(at3[u][:], picked(neg_h[t], n3_sb, a, b))
-
-        def top(u):
-            t, a, b = u
-            neg_top[u] = tile([P, b - a], F32, f"neg_top{t}_{a}")
-            nc.vector.tensor_tensor(neg_top[u][:], at3[u][:], neg_h[t][:, a:b], ALU.min)
-
-        def fetch_less(u, lists, into, name):
-            t, a, b = u
-            into[u] = tile([P, b - a], F32, f"{name}_{t}_{a}")
-            nc.vector.tensor_tensor(into[u][:], picked(neg_h[t], lists, a, b), neg_top[u][:], ALU.subtract)
+            into[u] = tile([P, b - a], F32, f"{name}_{t}_{a}" if t else reused)
+            nc.vector.tensor_tensor(into[u][:], picked(neg_h[t], lists, a, b), top[t][:, a:b], ALU.add if t else ALU.subtract)
 
         def finish_out(u):
             t, a, b = u
-            result = tile([P, b - a], F32, f"result{t}_{a}")
-            nc.vector.tensor_tensor(result[:], less4[u][:], less5[u][:], ALU.min)
-            nc.sync.dma_start(out_rows[:, t, a:b], result[:])
-            for (c, d), dst in zip(OUT_PIECES, out_bf):
-                if a <= c and d <= b:
-                    nc.scalar.copy(dst[:, :, t], result[:, c - a : d - a])
+            both = result[t // 2]
+            nc.vector.tensor_tensor(both[:, t % 2, a:b], less4[u][:], less5[u][:], ALU.min)
+            nc.sync.dma_start(out_rows[:, t, a:b], both[:, t % 2, a:b])
+            if t % 2:
+                for (c, d), dst in zip(OUT_PIECES, out_bf):
+                    if a <= c and d <= b:
+                        nc.scalar.copy(dst[:, :, t - 1 : t + 1], both[:, :, c:d].rearrange("p t n -> p n t"))
 
         def planes(i):
             a, b = OUT_PIECES[i]
@@ -216,21 +264,12 @@ def tile_picked_densekindmix_none_po_kernel(
             nc.vector.quantize_mx(codes[:].bitcast(FP8X4), out_scales[:, a:b], out_bf[i][:].rearrange("p n t -> p (n t)"))
             nc.sync.dma_start(words_of(out_1)[:, a:b], codes[:])
 
-        fetch3(second[0])
-        fetch3(second[1])
-        top(second[0])
-        top(second[1])
-        for u, ahead in zip(second, second[2:]):
-            fetch_less(u, n4_sb, less4, "less4")
-            fetch_less(u, n5_sb, less5, "less5")
-            fetch3(ahead)
+        fetch_less(second[0], n4_sb, less4, "less4", "h2")
+        for u, following in zip(second, second[1:]):
+            fetch_less(u, n5_sb, less5, "less5", "h3")
+            fetch_less(following, n4_sb, less4, "less4", "h2")
             finish_out(u)
-            top(ahead)
-        fetch_less(second[-2], n4_sb, less4, "less4")
-        fetch_less(second[-2], n5_sb, less5, "less5")
-        fetch_less(second[-1], n4_sb, less4, "less4")
-        finish_out(second[-2])
-        fetch_less(second[-1], n5_sb, less5, "less5")
+        fetch_less(second[-1], n5_sb, less5, "less5", "h3")
         planes(0)
         finish_out(second[-1])
         planes(1)

@@ -15,18 +15,24 @@ COPY = mybir.ActivationFunctionType.Copy
 RELU = mybir.ActivationFunctionType.Relu
 
 P = 128
-PACK = 4
+PLANES = 4
+LAST = PLANES - 1
 N = 512
+HALF = N // 2
 TABLE = 2048
 STRIPE = 16
+QUADRANTS = 4
+BANKS = 8
+LINE_WORDS = 4
+LINE_BYTES = 16
 FLOPS = 2 * 2 * 512 * 512 * 512
 
-Z_PIECES = ((0, 256), (256, 512))
-OUT_PIECES = ((0, 256), (256, 384), (384, 512))
+Z_PIECES = ((0, HALF), (HALF, N))
+OUT_PIECES = ((0, HALF), (HALF, 3 * P), (3 * P, N))
 
 
-def units(pieces):
-    return [(t, 0, N) for t in range(PACK - 1)] + [(PACK - 1, a, b) for a, b in pieces]
+def steps(pieces):
+    return [(t, 0, N) for t in range(LAST)] + [(LAST, a, b) for a, b in pieces]
 
 
 def tile_picked_densekindmix_none_po_kernel(
@@ -41,24 +47,31 @@ def tile_picked_densekindmix_none_po_kernel(
         def tile(shape, dtype, name):
             return keep.tile(shape, dtype, name=name, align_bytes=64)
 
+        def bank(number):
+            return psum.tile([P, N], F32, name=f"bank{number % BANKS}")
+
+        def window(t, name):
+            return tile([P, N if t == LAST else 2 * N], F32, name)
+
+        def picked(table, entries, a, b):
+            return table.indirect(entries[:, a // STRIPE : b // STRIPE])
+
         def load_list(dram, name):
-            held = tile([P, N // STRIPE], U16, name)
-            nc.sync.dma_start(held[:], dram)
-            return held
+            entries = tile([P, N // STRIPE], U16, name)
+            nc.sync.dma_start(entries[:], dram)
+            return entries
 
         def words_of(dram):
             return dram[0].rearrange("p n t -> p (n t)").bitcast(I32)
 
-        def window(t, name):
-            return tile([P, N if t == PACK - 1 else 2 * N], F32, name)
+        def load_scale_rows(dst, dram):
+            for q in range(QUADRANTS):
+                nc.sync.dma_start(dst[:].bitcast(I32)[32 * q : 32 * q + 4, :], dram[0].bitcast(I32)[4 * q : 4 * q + 4, :])
 
-        def picked(win, lists, a, b):
-            return win[:].indirect(lists[:, a // STRIPE : b // STRIPE])
-
-        def deal(dst, src, run, first=0, last=PACK):
+        def deal(dst, src, line, first=0, end=PLANES):
             nc.vector.tensor_copy(
-                dst.rearrange("p (t c m) -> p c t m", t=PACK, m=run)[:, :, first:last, :],
-                src.rearrange("p (c m t) -> p c t m", t=PACK, m=run)[:, :, first:last, :],
+                dst.rearrange("p (t c m) -> p c t m", t=PLANES, m=line)[:, :, first:end, :],
+                src.rearrange("p (c m t) -> p c t m", t=PLANES, m=line)[:, :, first:end, :],
             )
 
         xs_table = tile([P, TABLE], U8, "xs_table")
@@ -68,33 +81,26 @@ def tile_picked_densekindmix_none_po_kernel(
         xw_table = tile([P, TABLE], I32, "xw_table")
         dw_table = tile([P, TABLE], I32, "dw_table")
         w1w_raw = tile([P, N], I32, "w1w_raw")
-        gs_sb = tile([P, PACK], F32, "gs_sb")
-        tab_rows = tab.rearrange("(p t) j -> p t j", t=PACK)
-        tab_win = [window(t, f"tab_win{t}") for t in range(PACK)]
+        gs_sb = tile([P, PLANES], F32, "gs_sb")
+        tab_win = [window(t, f"tab_win{t}") for t in range(PLANES)]
         nc.gpsimd.memset(xs_table[:].bitcast(I32), 0)
         nc.vector.memset(w1s_raw[:].bitcast(I32), 0)
         nc.vector.memset(ds_table[:].bitcast(I32), 0)
         nc.vector.memset(ds_placed[:].bitcast(I32), 0)
+
         nc.sync.dma_start(w1w_raw[:], words_of(w1_words))
         offs_sb = load_list(offs, "offs_sb")
-        nc.sync.dma_start(xs_table[:].bitcast(I32)[0 : 4, :], x_scales[0].bitcast(I32)[0 : 4, :])
-        nc.sync.dma_start(xs_table[:].bitcast(I32)[32 : 36, :], x_scales[0].bitcast(I32)[4 : 8, :])
-        nc.sync.dma_start(xs_table[:].bitcast(I32)[64 : 68, :], x_scales[0].bitcast(I32)[8 : 12, :])
-        nc.sync.dma_start(xs_table[:].bitcast(I32)[96 : 100, :], x_scales[0].bitcast(I32)[12 : 16, :])
+        load_scale_rows(xs_table, x_scales)
         nc.sync.dma_start(xw_table[:], words_of(x_words))
-        nc.sync.dma_start(w1s_raw[:].bitcast(I32)[0 : 4, :], w1_scales[0].bitcast(I32)[0 : 4, :])
-        nc.sync.dma_start(w1s_raw[:].bitcast(I32)[32 : 36, :], w1_scales[0].bitcast(I32)[4 : 8, :])
-        nc.sync.dma_start(w1s_raw[:].bitcast(I32)[64 : 68, :], w1_scales[0].bitcast(I32)[8 : 12, :])
-        nc.sync.dma_start(w1s_raw[:].bitcast(I32)[96 : 100, :], w1_scales[0].bitcast(I32)[12 : 16, :])
+        load_scale_rows(w1s_raw, w1_scales)
         k1_sb = load_list(k1, "k1_sb")
         nc.sync.dma_start(ds_table[:].bitcast(I32)[0:P:8, :], d_scales[0].bitcast(I32))
         n2_sb = load_list(n2, "n2_sb")
         n1_sb = load_list(n1, "n1_sb")
-        nc.sync.dma_start(tab_win[0][:, 0:N], tab_rows[:, 0, :])
-        nc.sync.dma_start(tab_win[1][:, 0:N], tab_rows[:, 1, :])
-        nc.sync.dma_start(tab_win[2][:, 0:N], tab_rows[:, 2, :])
-        nc.sync.dma_start(tab_win[3][:, 0:N], tab_rows[:, 3, :])
-        nc.sync.dma_start(gs_sb[:], gs.rearrange("(p t) o -> p (t o)", t=PACK))
+        tab_planes = tab.rearrange("(p t) j -> p t j", t=PLANES)
+        for t in range(PLANES):
+            nc.sync.dma_start(tab_win[t][:, 0:N], tab_planes[:, t, :])
+        nc.sync.dma_start(gs_sb[:], gs.rearrange("(p t) o -> p (t o)", t=PLANES))
         nc.sync.dma_start(dw_table[:], words_of(d_words))
         n3_sb = load_list(n3, "n3_sb")
         n4_sb = load_list(n4, "n4_sb")
@@ -104,64 +110,66 @@ def tile_picked_densekindmix_none_po_kernel(
         make_identity(nc, identity[:])
 
         xs = tile([P, N], U8, "xs")
-        nc.vector.tensor_copy(xs[:], picked(xs_table, offs_sb, 0, N))
+        nc.vector.tensor_copy(xs[:], picked(xs_table[:], offs_sb, 0, N))
         w1w = tile([P, N], U32, "w1w")
-        deal(w1w[:], w1w_raw[:].bitcast(U32), 4)
+        deal(w1w[:], w1w_raw[:].bitcast(U32), LINE_WORDS)
         w1s = tile([P, N], U8, "w1s")
-        deal(w1s[:], w1s_raw[:], 16)
+        deal(w1s[:], w1s_raw[:], LINE_BYTES)
         xw = tile([P, N], U32, "xw")
-        nc.vector.tensor_copy(xw[:], xw_table[:].bitcast(U32).indirect(offs_sb[:]))
+        nc.vector.tensor_copy(xw[:], picked(xw_table[:].bitcast(U32), offs_sb, 0, N))
 
-        y_win = []
-        for t in range(PACK):
-            bank = psum.tile([P, N], F32, name=f"bank{t}")
-            cols = slice(t * P, (t + 1) * P)
-            nc.tensor.matmul_mx(bank[:], w1w[:, cols].bitcast(FP8X4), w1s[:, cols], xw[:].bitcast(FP8X4), xs[:], start=True, stop=True)
-            y_win.append(window(t, f"y_win{t}"))
-            nc.scalar.copy(y_win[t][:, 0:N], bank[:])
+        blocks = [slice(c * P, (c + 1) * P) for c in range(N // P)]
+        y_win = [window(t, f"y_win{t}") for t in range(PLANES)]
+        for t in range(PLANES):
+            acc = bank(t)
+            nc.tensor.matmul_mx(
+                acc[:], w1w[:, blocks[t]].bitcast(FP8X4), w1s[:, blocks[t]], xw[:].bitcast(FP8X4), xs[:], start=True, stop=True
+            )
+            nc.scalar.copy(y_win[t][:, 0:N], acc[:])
 
         ds_picked = tile([P, N], U8, "ds_picked")
-        nc.vector.tensor_copy(ds_picked[:], picked(ds_table, k1_sb, 0, N))
+        nc.vector.tensor_copy(ds_picked[:], picked(ds_table[:], k1_sb, 0, N))
         ds_dealt = tile([P, N], U8, "ds_dealt")
-        deal(ds_dealt[:], ds_picked[:], 16)
+        deal(ds_dealt[:], ds_picked[:], LINE_BYTES)
         for r in range(4):
             nc.sync.dma_start(ds_placed[:].bitcast(I32)[r:P:32, :], ds_dealt[:].bitcast(I32)[8 * r : P : 32, :])
 
-        z_bf = [tile([P, b - a, PACK], BF16, f"z_bf{a}") for a, b in Z_PIECES]
-        first = units(Z_PIECES)
-        other = {}
-        summed = {}
+        z_bf = [tile([P, b - a, PLANES], BF16, f"z_bf{a}") for a, b in Z_PIECES]
+        y_at_n2 = {}
+        y_plus_tab = {}
 
-        def fetch_other(u):
-            t, a, b = u
-            other[u] = tile([P, b - a], F32, f"other{t}_{a}")
-            nc.vector.tensor_copy(other[u][:], picked(y_win[t], n2_sb, a, b))
+        def fetch_n2(step):
+            t, a, b = step
+            y_at_n2[step] = tile([P, b - a], F32, f"y_at_n2_{t}_{a}")
+            nc.vector.tensor_copy(y_at_n2[step][:], picked(y_win[t][:], n2_sb, a, b))
 
-        def fetch_sum(u):
-            t, a, b = u
-            summed[u] = tile([P, b - a], F32, f"summed{t}_{a}")
-            nc.vector.tensor_tensor(summed[u][:], picked(tab_win[t], n1_sb, a, b), y_win[t][:, a:b], ALU.add)
+        def fetch_n1(step):
+            t, a, b = step
+            y_plus_tab[step] = tile([P, b - a], F32, f"y_plus_tab_{t}_{a}")
+            nc.vector.tensor_tensor(y_plus_tab[step][:], picked(tab_win[t][:], n1_sb, a, b), y_win[t][:, a:b], ALU.add)
 
-        def finish_z(u):
-            t, a, b = u
-            larger = tile([P, b - a], F32, f"larger{t}_{a}")
-            nc.vector.tensor_tensor(larger[:], summed[u][:], other[u][:], ALU.max)
+        def finish_z(step):
+            t, a, b = step
+            larger = tile([P, b - a], F32, f"larger_{t}_{a}")
+            nc.vector.tensor_tensor(larger[:], y_plus_tab[step][:], y_at_n2[step][:], ALU.max)
             for (c, d), dst in zip(Z_PIECES, z_bf):
                 if a <= c and d <= b:
                     nc.scalar.activation(dst[:, :, t], larger[:, c - a : d - a], COPY, scale=gs_sb[:, t : t + 1])
 
-        fetch_other(first[0])
-        for u, following in zip(first, first[1:]):
-            fetch_sum(u)
-            fetch_other(following)
-            if following != first[-1]:
-                finish_z(u)
-        fetch_sum(first[-1])
-        finish_z(first[-2])
-        finish_z(first[-1])
+        z_steps = steps(Z_PIECES)
+        fetch_n2(z_steps[0])
+        for step, following in zip(z_steps[:-2], z_steps[1:]):
+            fetch_n1(step)
+            fetch_n2(following)
+            finish_z(step)
+        fetch_n1(z_steps[-2])
+        fetch_n2(z_steps[-1])
+        fetch_n1(z_steps[-1])
+        finish_z(z_steps[-2])
+        finish_z(z_steps[-1])
 
         dw_picked = tile([P, N], U32, "dw_picked")
-        nc.vector.tensor_copy(dw_picked[:], dw_table[:].bitcast(U32).indirect(k1_sb[:]))
+        nc.vector.tensor_copy(dw_picked[:], picked(dw_table[:].bitcast(U32), k1_sb, 0, N))
         z_words = [tile([P, b - a], U32, f"z_words{a}") for a, b in Z_PIECES]
         z_scales = [tile([P, b - a], U8, f"z_scales{a}") for a, b in Z_PIECES]
 
@@ -170,110 +178,125 @@ def tile_picked_densekindmix_none_po_kernel(
 
         dw = tile([P, N], U32, "dw")
         quantize_z(0)
-        deal(dw[:], dw_picked[:], 4, 0, 1)
+        deal(dw[:], dw_picked[:], LINE_WORDS, 0, 1)
         quantize_z(1)
-        deal(dw[:], dw_picked[:], 4, 1, PACK)
+        deal(dw[:], dw_picked[:], LINE_WORDS, 1, PLANES)
 
-        neg_h = [window(t, f"neg_h{t}") for t in range(PACK)]
-        blocks = [slice(c * P, (c + 1) * P) for c in range(N // P)]
+        neg_h = [window(t, f"neg_h{t}") for t in range(PLANES)]
+        shortfall = {}
         h_turned = {}
         gain_turned = {}
-        gap3 = {}
         top = {}
 
         def product(t):
-            cols = slice(t * P, (t + 1) * P)
             for i, (a, b) in enumerate(Z_PIECES):
-                bank = psum.tile([P, N], F32, name=f"bank{(4 + 2 * t + i) % 8}")
-                nc.tensor.matmul_mx(bank[:, 0 : b - a], dw[:, cols].bitcast(FP8X4), ds_placed[:, cols], z_words[i][:].bitcast(FP8X4), z_scales[i][:], start=True, stop=True)
-                nc.scalar.activation(neg_h[t][:, a:b], bank[:, 0 : b - a], COPY, scale=-0.0625)
+                acc = bank(4 + 2 * t + i)
+                nc.tensor.matmul_mx(
+                    acc[:, 0 : b - a], dw[:, blocks[t]].bitcast(FP8X4), ds_placed[:, blocks[t]],
+                    z_words[i][:].bitcast(FP8X4), z_scales[i][:], start=True, stop=True,
+                )
+                nc.scalar.activation(neg_h[t][:, a:b], acc[:, 0 : b - a], COPY, scale=-0.0625)
 
-        def turn_h(t):
-            bank = psum.tile([P, N], F32, name=f"bank{(4 + 2 * t) % 8}")
-            for block in blocks:
-                nc.tensor.transpose(bank[:, block], neg_h[t][:, block], identity[:])
-            h_turned[t] = tile([P, N], F32, f"h_turned{t}")
-            nc.scalar.activation(h_turned[t][:], bank[:], COPY, scale=-1.0)
-
-        def fetch3(t):
+        def fetch_n3(t):
             h = tile([P, N], F32, f"h{t}")
             nc.scalar.activation(h[:], neg_h[t][:, 0:N], COPY, scale=-1.0)
-            gap3[t] = tile([P, N], F32, f"gap3_{t}")
-            for a, b in Z_PIECES if t == PACK - 1 else ((0, N),):
-                nc.vector.tensor_tensor(gap3[t][:, a:b], picked(neg_h[t], n3_sb, a, b), h[:, a:b], ALU.add)
+            shortfall[t] = tile([P, N], F32, f"shortfall{t}")
+            for a, b in Z_PIECES if t == LAST else ((0, N),):
+                nc.vector.tensor_tensor(shortfall[t][:, a:b], picked(neg_h[t][:], n3_sb, a, b), h[:, a:b], ALU.add)
 
-        def turn_gain(t):
-            bank = psum.tile([P, N], F32, name=f"bank{(5 + 2 * t) % 8}")
+        def turn_negated(src, bank_number, func, name):
+            acc = bank(bank_number)
             for block in blocks:
-                nc.tensor.transpose(bank[:, block], gap3[t][:, block], identity[:])
-            gain_turned[t] = tile([P, N], F32, f"gain_turned{t}")
-            nc.scalar.activation(gain_turned[t][:], bank[:], RELU, scale=-1.0)
+                nc.tensor.transpose(acc[:, block], src[:, block], identity[:])
+            turned = tile([P, N], F32, name)
+            nc.scalar.activation(turned[:], acc[:], func, scale=-1.0)
+            return turned
 
-        def make_top(t):
-            bank = psum.tile([P, N], F32, name=f"bank{(4 + 2 * t) % 8}")
+        def turn_terms(t):
+            h_turned[t] = turn_negated(neg_h[t], 4 + 2 * t, COPY, f"h_turned{t}")
+            gain_turned[t] = turn_negated(shortfall[t], 5 + 2 * t, RELU, f"gain_turned{t}")
+
+        def add_terms(t):
+            acc = bank(4 + 2 * t)
             for block in blocks:
-                nc.tensor.matmul(bank[:, block], h_turned[t][:, block], identity[:], start=True, stop=False, is_transpose=True)
-                nc.tensor.matmul(bank[:, block], gain_turned[t][:, block], identity[:], start=False, stop=True, is_transpose=True)
+                nc.tensor.matmul(acc[:, block], h_turned[t][:, block], identity[:], start=True, stop=False, is_transpose=True)
+                nc.tensor.matmul(acc[:, block], gain_turned[t][:, block], identity[:], start=False, stop=True, is_transpose=True)
             top[t] = tile([P, N], F32, f"top{t}")
-            nc.scalar.copy(top[t][:], bank[:])
+            nc.scalar.copy(top[t][:], acc[:])
 
         product(0)
-        at3 = tile([P, N], F32, "at3")
-        nc.vector.tensor_copy(at3[:], picked(neg_h[0], n3_sb, 0, N))
+        neg_h0_at_n3 = tile([P, N], F32, "neg_h0_at_n3")
+        nc.vector.tensor_copy(neg_h0_at_n3[:], picked(neg_h[0][:], n3_sb, 0, N))
         product(1)
-        fetch3(1)
-        top[0] = tile([P, N], F32, "neg_top0")
-        nc.vector.tensor_tensor(top[0][:], at3[:], neg_h[0][:, 0:N], ALU.min)
-        for t in range(2, PACK):
+        fetch_n3(1)
+        neg_top0 = tile([P, N], F32, "neg_top0")
+        nc.vector.tensor_tensor(neg_top0[:], neg_h0_at_n3[:], neg_h[0][:, 0:N], ALU.min)
+        for t in range(2, PLANES):
             product(t)
-            fetch3(t)
-        turn_h(1)
-        turn_gain(1)
-        for t in range(2, PACK):
-            turn_h(t)
-            turn_gain(t)
-            make_top(t - 1)
-        make_top(PACK - 1)
+            fetch_n3(t)
+        turn_terms(1)
+        for t in range(2, PLANES):
+            turn_terms(t)
+            add_terms(t - 1)
+        add_terms(LAST)
 
-        second = units(OUT_PIECES)
-        out_bf = [tile([P, b - a, PACK], BF16, name) for (a, b), name in zip(OUT_PIECES, ("gap3_3", "h_turned3", "gain_turned3"))]
+        spent = (f"shortfall{LAST}", f"h_turned{LAST}", f"gain_turned{LAST}")
+        out_bf = [tile([P, b - a, PLANES], BF16, name) for (a, b), name in zip(OUT_PIECES, spent)]
+        out_words = tile([P, N], I32, "out_words")
         out_scales = tile([P, N], U8, "out_scales")
-        out_rows = out_0.rearrange("(p t) j -> p t j", t=PACK)
-        result = [tile([P, 2, N], F32, f"result{pair}") for pair in range(2)]
-        less4 = {}
-        less5 = {}
+        out_planes = out_0.rearrange("(p t) j -> p t j", t=PLANES)
+        result = [tile([P, 2, N], F32, f"result{pair}") for pair in range(PLANES // 2)]
+        less_n4 = {}
+        less_n5 = {}
 
-        def fetch_less(u, lists, into, name, reused):
-            t, a, b = u
-            into[u] = tile([P, b - a], F32, f"{name}_{t}_{a}" if t else reused)
-            nc.vector.tensor_tensor(into[u][:], picked(neg_h[t], lists, a, b), top[t][:, a:b], ALU.add if t else ALU.subtract)
+        def fetch_less(step, entries, into, name, spent_h):
+            t, a, b = step
+            if t == 0:
+                into[step] = tile([P, N], F32, spent_h)
+                nc.vector.tensor_tensor(into[step][:], picked(neg_h[0][:], entries, 0, N), neg_top0[:], ALU.subtract)
+            else:
+                into[step] = tile([P, b - a], F32, f"{name}_{t}_{a}")
+                nc.vector.tensor_tensor(into[step][:], picked(neg_h[t][:], entries, a, b), top[t][:, a:b], ALU.add)
 
-        def finish_out(u):
-            t, a, b = u
-            both = result[t // 2]
-            nc.vector.tensor_tensor(both[:, t % 2, a:b], less4[u][:], less5[u][:], ALU.min)
-            nc.sync.dma_start(out_rows[:, t, a:b], both[:, t % 2, a:b])
+        def fetch_n4(step):
+            fetch_less(step, n4_sb, less_n4, "less_n4", "h2")
+
+        def fetch_n5(step):
+            fetch_less(step, n5_sb, less_n5, "less_n5", "h3")
+
+        def whole_halves(a, b):
+            return slice(a - a % HALF, b) if b % HALF == 0 else None
+
+        def finish_out(step):
+            t, a, b = step
+            pair = result[t // 2]
+            nc.vector.tensor_tensor(pair[:, t % 2, a:b], less_n4[step][:], less_n5[step][:], ALU.min)
+            cols = whole_halves(a, b)
+            if cols is not None:
+                nc.sync.dma_start(out_planes[:, t, cols], pair[:, t % 2, cols])
             if t % 2:
                 for (c, d), dst in zip(OUT_PIECES, out_bf):
                     if a <= c and d <= b:
-                        nc.scalar.copy(dst[:, :, t - 1 : t + 1], both[:, :, c:d].rearrange("p t n -> p n t"))
+                        nc.scalar.copy(dst[:, :, t - 1 : t + 1], pair[:, :, c:d].rearrange("p t n -> p n t"))
 
-        def planes(i):
+        def quantize_out(i):
             a, b = OUT_PIECES[i]
-            codes = tile([P, b - a], I32, f"out_words{a}")
-            nc.vector.quantize_mx(codes[:].bitcast(FP8X4), out_scales[:, a:b], out_bf[i][:].rearrange("p n t -> p (n t)"))
-            nc.sync.dma_start(words_of(out_1)[:, a:b], codes[:])
+            nc.vector.quantize_mx(out_words[:, a:b].bitcast(FP8X4), out_scales[:, a:b], out_bf[i][:].rearrange("p n t -> p (n t)"))
+            cols = whole_halves(a, b)
+            if cols is not None:
+                nc.sync.dma_start(words_of(out_1)[:, cols], out_words[:, cols])
 
-        fetch_less(second[0], n4_sb, less4, "less4", "h2")
-        for u, following in zip(second, second[1:]):
-            fetch_less(u, n5_sb, less5, "less5", "h3")
-            fetch_less(following, n4_sb, less4, "less4", "h2")
-            finish_out(u)
-        fetch_less(second[-1], n5_sb, less5, "less5", "h3")
-        planes(0)
-        finish_out(second[-1])
-        planes(1)
-        planes(2)
-        for q in range(4):
+        out_steps = steps(OUT_PIECES)
+        fetch_n4(out_steps[0])
+        for step, following in zip(out_steps, out_steps[1:]):
+            fetch_n5(step)
+            fetch_n4(following)
+            finish_out(step)
+        fetch_n5(out_steps[-1])
+        quantize_out(0)
+        finish_out(out_steps[-1])
+        quantize_out(1)
+        quantize_out(2)
+        for q in range(QUADRANTS):
             queue = nc.scalar if q % 2 else nc.sync
             queue.dma_start(out_2[0].bitcast(I32)[4 * q : 4 * q + 4, :], out_scales[:].bitcast(I32)[32 * q : 32 * q + 4, :])

from contextlib import ExitStack

import concourse.mybir as mybir
from concourse.masks import make_identity

F32 = mybir.dt.float32
BF16 = mybir.dt.bfloat16
I32 = mybir.dt.int32
U32 = mybir.dt.uint32
U16 = mybir.dt.uint16
U8 = mybir.dt.uint8
FP8X4 = mybir.dt.float8_e4m3fn_x4
ALU = mybir.AluOpType
COPY = mybir.ActivationFunctionType.Copy
RELU = mybir.ActivationFunctionType.Relu

P = 128
PLANES = 4
LAST = PLANES - 1
N = 512
HALF = N // 2
TABLE = 2048
STRIPE = 16
QUADRANTS = 4
BANKS = 8
LINE_WORDS = 4
LINE_BYTES = 16
FLOPS = 2 * 2 * 512 * 512 * 512

Z_PIECES = ((0, HALF), (HALF, N))
OUT_PIECES = ((0, HALF), (HALF, 3 * P), (3 * P, N))


def steps(pieces):
    return [(t, 0, N) for t in range(LAST)] + [(LAST, a, b) for a, b in pieces]


def tile_picked_densekindmix_none_po_kernel(
    tc, x_words, x_scales, w1_words, w1_scales, tab, gs, d_words, d_scales,
    offs, n1, n2, k1, n3, n4, n5, out_0, out_1, out_2,
):
    nc = tc.nc
    with ExitStack() as ctx:
        keep = ctx.enter_context(tc.tile_pool(name="keep", bufs=1))
        psum = ctx.enter_context(tc.psum_pool(name="psum", bufs=1))

        def tile(shape, dtype, name):
            return keep.tile(shape, dtype, name=name, align_bytes=64)

        def bank(number):
            return psum.tile([P, N], F32, name=f"bank{number % BANKS}")

        def window(t, name):
            return tile([P, N if t == LAST else 2 * N], F32, name)

        def picked(table, entries, a, b):
            return table.indirect(entries[:, a // STRIPE : b // STRIPE])

        def load_list(dram, name):
            entries = tile([P, N // STRIPE], U16, name)
            nc.sync.dma_start(entries[:], dram)
            return entries

        def words_of(dram):
            return dram[0].rearrange("p n t -> p (n t)").bitcast(I32)

        def load_scale_rows(dst, dram):
            for q in range(QUADRANTS):
                nc.sync.dma_start(dst[:].bitcast(I32)[32 * q : 32 * q + 4, :], dram[0].bitcast(I32)[4 * q : 4 * q + 4, :])

        def deal(dst, src, line, first=0, end=PLANES):
            nc.vector.tensor_copy(
                dst.rearrange("p (t c m) -> p c t m", t=PLANES, m=line)[:, :, first:end, :],
                src.rearrange("p (c m t) -> p c t m", t=PLANES, m=line)[:, :, first:end, :],
            )

        xs_table = tile([P, TABLE], U8, "xs_table")
        ds_table = tile([P, TABLE], U8, "ds_table")
        w1s_raw = tile([P, N], U8, "w1s_raw")
        ds_placed = tile([P, N], U8, "ds_placed")
        xw_table = tile([P, TABLE], I32, "xw_table")
        dw_table = tile([P, TABLE], I32, "dw_table")
        w1w_raw = tile([P, N], I32, "w1w_raw")
        gs_sb = tile([P, PLANES], F32, "gs_sb")
        tab_win = [window(t, f"tab_win{t}") for t in range(PLANES)]
        nc.gpsimd.memset(xs_table[:].bitcast(I32), 0)
        nc.vector.memset(w1s_raw[:].bitcast(I32), 0)
        nc.vector.memset(ds_table[:].bitcast(I32), 0)
        nc.vector.memset(ds_placed[:].bitcast(I32), 0)

        nc.sync.dma_start(w1w_raw[:], words_of(w1_words))
        offs_sb = load_list(offs, "offs_sb")
        load_scale_rows(xs_table, x_scales)
        nc.sync.dma_start(xw_table[:], words_of(x_words))
        load_scale_rows(w1s_raw, w1_scales)
        k1_sb = load_list(k1, "k1_sb")
        nc.sync.dma_start(ds_table[:].bitcast(I32)[0:P:8, :], d_scales[0].bitcast(I32))
        n2_sb = load_list(n2, "n2_sb")
        n1_sb = load_list(n1, "n1_sb")
        tab_planes = tab.rearrange("(p t) j -> p t j", t=PLANES)
        for t in range(PLANES):
            nc.sync.dma_start(tab_win[t][:, 0:N], tab_planes[:, t, :])
        nc.sync.dma_start(gs_sb[:], gs.rearrange("(p t) o -> p (t o)", t=PLANES))
        nc.sync.dma_start(dw_table[:], words_of(d_words))
        n3_sb = load_list(n3, "n3_sb")
        n4_sb = load_list(n4, "n4_sb")
        n5_sb = load_list(n5, "n5_sb")

        identity = tile([P, P], F32, "identity")
        make_identity(nc, identity[:])

        xs = tile([P, N], U8, "xs")
        nc.vector.tensor_copy(xs[:], picked(xs_table[:], offs_sb, 0, N))
        w1w = tile([P, N], U32, "w1w")
        deal(w1w[:], w1w_raw[:].bitcast(U32), LINE_WORDS)
        w1s = tile([P, N], U8, "w1s")
        deal(w1s[:], w1s_raw[:], LINE_BYTES)
        xw = tile([P, N], U32, "xw")
        nc.vector.tensor_copy(xw[:], picked(xw_table[:].bitcast(U32), offs_sb, 0, N))

        blocks = [slice(c * P, (c + 1) * P) for c in range(N // P)]
        y_win = [window(t, f"y_win{t}") for t in range(PLANES)]
        for t in range(PLANES):
            acc = bank(t)
            nc.tensor.matmul_mx(
                acc[:], w1w[:, blocks[t]].bitcast(FP8X4), w1s[:, blocks[t]], xw[:].bitcast(FP8X4), xs[:], start=True, stop=True
            )
            nc.scalar.copy(y_win[t][:, 0:N], acc[:])

        ds_picked = tile([P, N], U8, "ds_picked")
        nc.vector.tensor_copy(ds_picked[:], picked(ds_table[:], k1_sb, 0, N))
        ds_dealt = tile([P, N], U8, "ds_dealt")
        deal(ds_dealt[:], ds_picked[:], LINE_BYTES)
        for r in range(4):
            nc.sync.dma_start(ds_placed[:].bitcast(I32)[r:P:32, :], ds_dealt[:].bitcast(I32)[8 * r : P : 32, :])

        z_bf = [tile([P, b - a, PLANES], BF16, f"z_bf{a}") for a, b in Z_PIECES]
        y_at_n2 = {}
        y_plus_tab = {}

        def fetch_n2(step):
            t, a, b = step
            y_at_n2[step] = tile([P, b - a], F32, f"y_at_n2_{t}_{a}")
            nc.vector.tensor_copy(y_at_n2[step][:], picked(y_win[t][:], n2_sb, a, b))

        def fetch_n1(step):
            t, a, b = step
            y_plus_tab[step] = tile([P, b - a], F32, f"y_plus_tab_{t}_{a}")
            nc.vector.tensor_tensor(y_plus_tab[step][:], picked(tab_win[t][:], n1_sb, a, b), y_win[t][:, a:b], ALU.add)

        def finish_z(step):
            t, a, b = step
            larger = tile([P, b - a], F32, f"larger_{t}_{a}")
            nc.vector.tensor_tensor(larger[:], y_plus_tab[step][:], y_at_n2[step][:], ALU.max)
            for (c, d), dst in zip(Z_PIECES, z_bf):
                if a <= c and d <= b:
                    nc.scalar.activation(dst[:, :, t], larger[:, c - a : d - a], COPY, scale=gs_sb[:, t : t + 1])

        z_steps = steps(Z_PIECES)
        fetch_n2(z_steps[0])
        for step, following in zip(z_steps[:-2], z_steps[1:]):
            fetch_n1(step)
            fetch_n2(following)
            finish_z(step)
        fetch_n1(z_steps[-2])
        fetch_n2(z_steps[-1])
        fetch_n1(z_steps[-1])
        finish_z(z_steps[-2])
        finish_z(z_steps[-1])

        dw_picked = tile([P, N], U32, "dw_picked")
        nc.vector.tensor_copy(dw_picked[:], picked(dw_table[:].bitcast(U32), k1_sb, 0, N))
        z_words = [tile([P, b - a], U32, f"z_words{a}") for a, b in Z_PIECES]
        z_scales = [tile([P, b - a], U8, f"z_scales{a}") for a, b in Z_PIECES]

        def quantize_z(i):
            nc.vector.quantize_mx(z_words[i][:].bitcast(FP8X4), z_scales[i][:], z_bf[i][:].rearrange("p n t -> p (n t)"))

        dw = tile([P, N], U32, "dw")
        quantize_z(0)
        deal(dw[:], dw_picked[:], LINE_WORDS, 0, 1)
        quantize_z(1)
        deal(dw[:], dw_picked[:], LINE_WORDS, 1, PLANES)

        neg_h = [window(t, f"neg_h{t}") for t in range(PLANES)]
        shortfall = {}
        h_turned = {}
        gain_turned = {}
        top = {}

        def product(t):
            for i, (a, b) in enumerate(Z_PIECES):
                acc = bank(4 + 2 * t + i)
                nc.tensor.matmul_mx(
                    acc[:, 0 : b - a], dw[:, blocks[t]].bitcast(FP8X4), ds_placed[:, blocks[t]],
                    z_words[i][:].bitcast(FP8X4), z_scales[i][:], start=True, stop=True,
                )
                nc.scalar.activation(neg_h[t][:, a:b], acc[:, 0 : b - a], COPY, scale=-0.0625)

        def fetch_n3(t):
            h = tile([P, N], F32, f"h{t}")
            nc.scalar.activation(h[:], neg_h[t][:, 0:N], COPY, scale=-1.0)
            shortfall[t] = tile([P, N], F32, f"shortfall{t}")
            for a, b in Z_PIECES if t == LAST else ((0, N),):
                nc.vector.tensor_tensor(shortfall[t][:, a:b], picked(neg_h[t][:], n3_sb, a, b), h[:, a:b], ALU.add)

        def turn_negated(src, bank_number, func, name):
            acc = bank(bank_number)
            for block in blocks:
                nc.tensor.transpose(acc[:, block], src[:, block], identity[:])
            turned = tile([P, N], F32, name)
            nc.scalar.activation(turned[:], acc[:], func, scale=-1.0)
            return turned

        def turn_terms(t):
            h_turned[t] = turn_negated(neg_h[t], 4 + 2 * t, COPY, f"h_turned{t}")
            gain_turned[t] = turn_negated(shortfall[t], 5 + 2 * t, RELU, f"gain_turned{t}")

        def add_terms(t):
            acc = bank(4 + 2 * t)
            for block in blocks:
                nc.tensor.matmul(acc[:, block], h_turned[t][:, block], identity[:], start=True, stop=False, is_transpose=True)
                nc.tensor.matmul(acc[:, block], gain_turned[t][:, block], identity[:], start=False, stop=True, is_transpose=True)
            top[t] = tile([P, N], F32, f"top{t}")
            nc.scalar.copy(top[t][:], acc[:])

        product(0)
        neg_h0_at_n3 = tile([P, N], F32, "neg_h0_at_n3")
        nc.vector.tensor_copy(neg_h0_at_n3[:], picked(neg_h[0][:], n3_sb, 0, N))
        product(1)
        fetch_n3(1)
        neg_top0 = tile([P, N], F32, "neg_top0")
        nc.vector.tensor_tensor(neg_top0[:], neg_h0_at_n3[:], neg_h[0][:, 0:N], ALU.min)
        for t in range(2, PLANES):
            product(t)
            fetch_n3(t)
        turn_terms(1)
        for t in range(2, PLANES):
            turn_terms(t)
            add_terms(t - 1)
        add_terms(LAST)

        spent = (f"shortfall{LAST}", f"h_turned{LAST}", f"gain_turned{LAST}")
        out_bf = [tile([P, b - a, PLANES], BF16, name) for (a, b), name in zip(OUT_PIECES, spent)]
        out_words = tile([P, N], I32, "out_words")
        out_scales = tile([P, N], U8, "out_scales")
        out_planes = out_0.rearrange("(p t) j -> p t j", t=PLANES)
        result = [tile([P, 2, N], F32, f"result{pair}") for pair in range(PLANES // 2)]
        less_n4 = {}
        less_n5 = {}

        def fetch_less(step, entries, into, name, spent_h):
            t, a, b = step
            if t == 0:
                into[step] = tile([P, N], F32, spent_h)
                nc.vector.tensor_tensor(into[step][:], picked(neg_h[0][:], entries, 0, N), neg_top0[:], ALU.subtract)
            else:
                into[step] = tile([P, b - a], F32, f"{name}_{t}_{a}")
                nc.vector.tensor_tensor(into[step][:], picked(neg_h[t][:], entries, a, b), top[t][:, a:b], ALU.add)

        def fetch_n4(step):
            fetch_less(step, n4_sb, less_n4, "less_n4", "h2")

        def fetch_n5(step):
            fetch_less(step, n5_sb, less_n5, "less_n5", "h3")

        def whole_halves(a, b):
            return slice(a - a % HALF, b) if b % HALF == 0 else None

        def finish_out(step):
            t, a, b = step
            pair = result[t // 2]
            nc.vector.tensor_tensor(pair[:, t % 2, a:b], less_n4[step][:], less_n5[step][:], ALU.min)
            cols = whole_halves(a, b)
            if cols is not None:
                nc.sync.dma_start(out_planes[:, t, cols], pair[:, t % 2, cols])
            if t % 2:
                for (c, d), dst in zip(OUT_PIECES, out_bf):
                    if a <= c and d <= b:
                        nc.scalar.copy(dst[:, :, t - 1 : t + 1], pair[:, :, c:d].rearrange("p t n -> p n t"))

        def quantize_out(i):
            a, b = OUT_PIECES[i]
            nc.vector.quantize_mx(out_words[:, a:b].bitcast(FP8X4), out_scales[:, a:b], out_bf[i][:].rearrange("p n t -> p (n t)"))
            cols = whole_halves(a, b)
            if cols is not None:
                nc.sync.dma_start(words_of(out_1)[:, cols], out_words[:, cols])

        out_steps = steps(OUT_PIECES)
        fetch_n4(out_steps[0])
        for step, following in zip(out_steps, out_steps[1:]):
            fetch_n5(step)
            fetch_n4(following)
            finish_out(step)
        fetch_n5(out_steps[-1])
        quantize_out(0)
        finish_out(out_steps[-1])
        quantize_out(1)
        quantize_out(2)
        for q in range(QUADRANTS):
            queue = nc.scalar if q % 2 else nc.sync
            queue.dma_start(out_2[0].bitcast(I32)[4 * q : 4 * q + 4, :], out_scales[:].bitcast(I32)[32 * q : 32 * q + 4, :])
